import numpy as np, ml_dtypes
CORES = [6,15,38,47]
N = 4
BF = ml_dtypes.bfloat16
def gentries(a):
    return np.ascontiguousarray(a.reshape(8, 16, -1).transpose(0, 2, 1)).reshape(8, -1)
def gtable(e):
    e = np.asarray(e); return np.ascontiguousarray(e.reshape(8, -1, 16).transpose(0, 2, 1)).reshape(128, -1).astype(np.int32)
ND, D, V, Q, TOP = 2048, 6, 320, 512, 1000000
def free(rng):
    s = rng.integers(-TOP, TOP + 1, (8, N * ND, 16))
    c = np.stack([rng.integers(0, (e + 1) * ND, (8, ND, 2)) for e in range(N)], 1).reshape(8, N * ND, 2)
    return s, c
def ledgers(rng):
    s, c = free(rng); G = np.arange(8); roots = []
    ids = np.stack([e * ND + np.argsort(rng.random((8, ND)), 1) for e in range(N)])
    a = rng.integers(-1000, 1001, (8, 1 << D, 16))
    for l in range(D):
        h = 1 << l; n = ids[0][:, h - 1:2 * h - 1]
        s[G[:, None], n] = np.add.reduce(a.reshape(8, h, 2, 1 << (D - 1 - l), 16)[:, :, 0], axis=2)
        if l < D - 1: c[G[:, None], n] = ids[0][:, 2 * h - 1:4 * h - 1].reshape(8, h, 2)
    cur = ids[0][:, 0]
    for e in range(N):
        k = (1 << D) - 1 if e == 0 else 0
        for i in range(V):
            t = rng.integers(0, 1 << D, 8); p = rng.integers(-300, 301, (8, 16)); old = cur; cur = ids[e][:, k]
            for l in range(D):
                b = (t >> (D - 1 - l)) & 1; n = ids[e][:, k]; k += 1
                s[G, n] = s[G, old] + (1 - b)[:, None] * p
                c[G, n] = c[G, old]
                if l < D - 1:
                    old = c[G, old, b]; c[G, n, b] = ids[e][:, k]
            roots.append(cur)
    return s, c, np.stack(roots)
def pack(s, c, ver, day):
    return {"sums": np.ascontiguousarray(s.reshape(8, N, ND, 16).transpose(1, 0, 3, 2)).reshape(N, 128, ND).astype(np.float32),
            "child": np.ascontiguousarray(c.reshape(8, N, 2 * ND).transpose(1, 0, 2)).astype(np.int32),
            "ver": np.stack([gtable(u) for u in ver]), "day": np.stack([gtable(u) for u in day])}
def setup_inputs(rng):
    s, c, roots = ledgers(rng)
    ver = roots[rng.integers(0, N * V, (N, 8, Q)), np.arange(8)[None, :, None]]
    return pack(s, c, ver, rng.integers(0, 1 << D, (N, 8, Q)))
def setup_inputs_any(rng):
    s, c = free(rng)
    return pack(s, c, rng.integers(0, N * ND, (N, 8, Q)), rng.integers(0, 1 << D, (N, 8, Q)))
def setup_inputs_ends(rng):
    s, c = free(rng); e = np.array([0, 1, ND - 2, ND - 1])
    s[:, :, :4] = TOP; s[:, :, 4:8] = -TOP
    c = np.stack([rng.integers(0, q + 1, (8, ND, 2)) * ND + rng.choice(e, (8, ND, 2)) for q in range(N)], 1).reshape(8, N * ND, 2)
    ver = rng.integers(0, N, (N, 8, Q)) * ND + rng.choice(e, (N, 8, Q))
    day = rng.choice(np.array([0, 0, (1 << D) - 1, (1 << D) - 1, (1 << D) - 2] + [1 << l for l in range(D)]), (N, 8, Q))
    ver[:, :, 0] = 0; ver[:, :, Q - 1] = N * ND - 1; day[:, :, 0] = 0; day[:, :, Q - 1] = (1 << D) - 1; day[:, :, 1] = 1; day[:, :, 2] = 1 << (D - 1)
    return pack(s, c, ver, day)
def setup_inputs_crowd(rng):
    s, c = free(rng); q = rng.integers(0, N); p = (q + rng.integers(1, N)) % N
    c[:, q * ND:(q + 1) * ND] = rng.integers(q * ND, (q + 1) * ND, (8, ND, 2))
    ver = rng.integers(q * ND, (q + 1) * ND, (N, 8, Q)); day = rng.integers(0, 1 << D, (N, 8, Q))
    ver[p] = ver[p][:, :1].copy(); day[p] = day[p][:, :1].copy() | 1
    day[p, 0] = (1 << D) - 1; day[p, 7] = (1 << D) - 1
    return pack(s, c, ver, day)
def setup_inputs_older(rng):
    s, c = free(rng)
    for e in range(1, N): c[:, e * ND:(e + 1) * ND] = rng.integers((e - 1) * ND, e * ND, (8, ND, 2))
    c[:, :ND] = np.where(rng.random((8, ND, 2)) < 0.5, np.arange(ND)[None, :, None], c[:, :ND])
    return pack(s, c, rng.integers((N - 1) * ND, N * ND, (N, 8, Q)), rng.integers(0, 1 << D, (N, 8, Q)))
def setup_inputs_spread(rng):
    d = setup_inputs(rng)
    v = rng.integers(-TOP, TOP + 1, (N, 128, ND)) >> (rng.integers(0, 17, (N, 1, ND)) + rng.integers(0, 4, (N, 128, 1)))
    d["sums"] = (v * (rng.random((N, 1, ND)) > 0.0625)).astype(np.float32); return d
def check_inputs(d):
    bad = []; s, c, v, t = d["sums"], d["child"], d["ver"], d["day"]
    if not (np.isfinite(s).all() and (np.abs(s) <= TOP).all() and (s == np.floor(s)).all()): bad.append("sums")
    if not ((c >= 0) & (c < ((np.arange(N) + 1) * ND)[:, None, None])).all(): bad.append("child")
    if not ((v >= 0) & (v < N * ND)).all(): bad.append("ver")
    if not ((t >= 0) & (t < (1 << D))).all(): bad.append("day")
    return bad
def reference(sums, child, ver, day):
    s = np.ascontiguousarray(sums.reshape(N, 8, 16, ND).transpose(1, 0, 3, 2)).reshape(8, N * ND, 16).astype(np.float64)
    c = np.ascontiguousarray(child.transpose(1, 0, 2)).reshape(8, 2 * N * ND).astype(np.int64)
    g = np.arange(8)[:, None]; y = np.zeros((N, 8, Q, 16), np.float64)
    for r in range(N):
        n = gentries(ver[r]).astype(np.int64); t = gentries(day[r]).astype(np.int64)
        for l in range(D - 1, -1, -1):
            b = (t >> l) & 1
            y[r] += b[:, :, None] * s[g, n]
            n = c[g, 2 * n + b]
    return {"y": np.ascontiguousarray(y.transpose(0, 1, 3, 2)).reshape(N, 128, Q).astype(np.float32)}

@@ -1,0 +1,313 @@
+from concourse.bass import DstId, RemoteDMATransfer
+from concourse.mybir import AluOpType as A, ActivationFunctionType as F
+
+ND = 2048
+BIG = 16384.0
+HUGE = 65536.0
+ZCOL = 8192
+PIECES = [(0, 128), (1, 320), (2, 320), (0, 384), (1, 320), (2, 320), (0, 256)]
+
+SCRATCH = {
+    "swin": ("sbuf", [128, 8200], "float32"),
+    "ctab": ("sbuf", [128, 16384], "bfloat16"),
+    "land": ("sbuf", [128, 2048], "bfloat16"),
+    "chi": ("sbuf", [128, 256], "int32"),
+    "zt": ("sbuf", [128, 512], "bfloat16"),
+    "verb": ("sbuf", [128, 32], "int32"),
+    "dayb": ("sbuf", [128, 32], "int32"),
+    "pidx": ("sbuf", [128, 4], "int32"),
+    "pint": ("sbuf", [128, 4], "int32"),
+    "pflt": ("sbuf", [128, 4], "float32"),
+    "ioi": ("sbuf", [128, 256], "float32"),
+    "iom": ("sbuf", [128, 128], "float32"),
+    "iod": ("sbuf", [128, 128], "float32"),
+    "bd": ("sbuf", [128, 128], "bfloat16"),
+    "ident": ("sbuf", [128, 128], "float32"),
+    "sa": ("sbuf", [128, 256], "float32"),
+    "sb": ("sbuf", [128, 256], "float32"),
+    "spat": ("sbuf", [128, 512], "float32"),
+    "bits": ("sbuf", [128, 192], "int32"),
+    "kk": ("sbuf", [128, 192], "float32"),
+    "t0": ("sbuf", [128, 32], "float32"),
+    "s0": ("sbuf", [128, 32], "float32"),
+    "uu": ("sbuf", [128, 192], "float32"),
+    "woff": ("sbuf", [128, 160], "uint16"),
+    "soff": ("sbuf", [128, 192], "uint16"),
+    "gat": ("sbuf", [128, 512], "bfloat16"),
+    "scn": ("sbuf", [128, 2560], "float32"),
+    "gs": ("sbuf", [128, 1536], "float32"),
+    "acc": ("sbuf", [128, 512], "float32"),
+    "ysb": ("sbuf", [128, 512], "float32"),
+    "pw0": ("psum", [128, 512], "float32"),
+    "pw1": ("psum", [128, 512], "float32"),
+    "pa0": ("psum", [128, 512], "float32"),
+    "pa1": ("psum", [128, 512], "float32"),
+}
+SEMAPHORES = (["v", "s", "p", "gi", "ldc", "ldv", "rl", "sarr", "lsem", "st"]
+              + ["ld%d" % k for k in range(len(PIECES))]
+              + ["h%d" % k for k in range(len(PIECES))]
+              + ["c%d" % k for k in range(4)])
+
+
+def bits_of(engs):
+    m = 0
+    for e in engs:
+        m |= 1 << e
+    return m
+
+
+def layout(T, topo, r):
+    me = T.cores[r]
+    mate = plane = far = None
+    for q, c in enumerate(T.cores):
+        if q == r:
+            continue
+        if topo.mates(topo.chip(me), topo.chip(c)):
+            mate = q
+        elif topo.same_plane(topo.chip(me), topo.chip(c)):
+            plane = q
+        else:
+            far = q
+    others = [c for c in topo.cores_of(me) if c != me]
+    port = [c for c in others if topo.may_write(c, T.cores[mate])]
+    port.sort(key=lambda c: topo.die(c) != topo.die(me))
+    rest = [c for c in others if c not in port]
+    side = []
+    for c in port:
+        d = [x for x in rest if topo.die(x) == topo.die(c) and x not in side][0]
+        side.append(d)
+    off = topo.engines(me, T.cores[mate])
+    spare = [e for e in topo.engines(me, others[0]) if e not in off]
+    return mate, plane, far, port, side, spare
+
+
+def dst(topo, c):
+    rid, pid, _ = topo.addr(c)
+    return DstId(rid=rid, pnc=pid)
+
+
+def piece_cols(r):
+    out, a = [], r * ND
+    for h, w in PIECES:
+        out.append((h, a, a + w))
+        a += w
+    return out
+
+
+def helper_program(g, core, T, topo):
+    sem = T.sem
+    for r, me in enumerate(T.cores):
+        if topo.chip(me) != topo.chip(core):
+            continue
+        mate, plane, far, port, side, spare = layout(T, topo, r)
+        n = 0
+        for k, (h, a, b) in enumerate(piece_cols(r)):
+            ap = T.swin[:, a:b]
+            if core == port[h]:
+                g.wait_ge(sem["h%d" % k], len(spare))
+                m = topo.mask(core, T.cores[mate])
+                g.remote_dma_fused([
+                    RemoteDMATransfer(dst_ids=[dst(topo, T.cores[far]), dst(topo, T.cores[mate])], dma_engine_mask=m,
+                                      remote_sem=sem.sarr, srcs=[ap], dsts=[ap, ap]),
+                    RemoteDMATransfer(dst_ids=[dst(topo, side[h])], dma_engine_mask=bits_of(spare),
+                                      remote_sem=sem["h%d" % k], srcs=[ap], dsts=[ap]),
+                ], local_sem=sem.lsem)
+                n += len(topo.engines(core, T.cores[mate])) + len(spare)
+            elif core == side[h]:
+                g.wait_ge(sem["h%d" % k], len(spare))
+                rid, pid, _ = topo.addr(T.cores[plane])
+                g.remote_dma(ap, ap, sem.sarr, sem.lsem, pid, rid, topo.mask(core, T.cores[plane]))
+                n += len(topo.engines(core, T.cores[plane]))
+        if n:
+            g.wait_ge(sem.lsem, n)
+
+
+def rank_program(g, core, T, topo):
+    r = T.rank_of(core)
+    if r is None:
+        helper_program(g, core, T, topo)
+        return
+    sem = T.sem
+    V, S, P, Y = g.vector, g.scalar, g.tensor, g.sync
+    mate, plane, far, port, side, spare = layout(T, topo, r)
+    noff = len(topo.engines(core, T.cores[mate]))
+    pcs = piece_cols(r)
+    cnt = {"v": 0, "s": 0, "p": 0, "gi": 0}
+
+    def inc(ins, name):
+        ins.then_inc(sem[name], 1)
+        cnt[name] += 1
+        return cnt[name]
+
+    def v(ins):
+        return inc(ins, "v")
+
+    def vw(n):
+        V.wait_ge(sem.v, n)
+
+    def quarter(e, a=0, b=4096):
+        return T.ctab[:, e * 4096 + a:e * 4096 + b]
+
+    Y.dma_start(T.chi[:], T.child[:]).then_inc(sem.ldc, 16)
+    for k, (h, a, b) in enumerate(pcs):
+        q = S if k % 2 == 0 else Y
+        q.dma_start(T.swin[:, a:b], T.sums[:, a - r * ND:b - r * ND]).then_inc(sem["ld%d" % k], 16)
+    Y.dma_start(T.verb[:], T.ver[:]).then_inc(sem.ldv, 16)
+    Y.dma_start(T.dayb[:], T.day[:]).then_inc(sem.ldv, 16)
+
+    inc(g.iota(T.pidx[:, 0:1], [[0, 1]], 0, 1), "gi")
+    inc(g.iota(T.ioi[:], [[0, 16], [1, 16]], 0, 0, allow_small_or_imprecise_dtypes=True), "gi")
+    gi_a = inc(g.iota(T.iom[:], [[1, 8], [0, 16]], 0, 0, allow_small_or_imprecise_dtypes=True), "gi")
+
+    n_z = v(V.memset(T.zt[:], 0.0))
+    n_qa = v(V.memset(quarter(far), 0.0))
+    V.wait_ge(sem.ldc, 16)
+    own = r * 512
+    n = v(V.tensor_copy(T.land[:, own:own + 256], T.chi[:]))
+    vw(n)
+    n_prep = v(V.tensor_tensor(T.land[:, own + 256:own + 512], T.chi[:], T.land[:, own:own + 256], A.subtract))
+    n_qo = v(V.memset(quarter(r, 0, 2048), 0.0))
+    n_qb = v(V.memset(quarter(plane), 0.0))
+    v(V.memset(T.swin[:, ZCOL:ZCOL + 8], 0.0))
+
+    S.wait_ge(sem.v, n_z)
+    for j in range(4):
+        s_qo = inc(S.activation(quarter(r, 2048 + 512 * j, 2560 + 512 * j), T.zt[:], F.Copy), "s")
+    for j in range(8):
+        s_qc = inc(S.activation(quarter(mate, 512 * j, 512 * j + 512), T.zt[:], F.Copy), "s")
+
+    nl = 0
+
+    def send_piece(k):
+        h, a, b = pcs[k]
+        g.wait_ge(sem["ld%d" % k], 16)
+        rid, pid, _ = topo.addr(port[h])
+        g.remote_dma(T.swin[:, a:b], T.swin[:, a:b], sem["h%d" % k], sem.lsem, pid, rid, bits_of(spare))
+
+    send_piece(0)
+    g.wait_ge(sem.v, n_prep)
+    for q in (far, plane, mate):
+        rid, pid, _ = topo.addr(T.cores[q])
+        ap = T.land[:, own:own + 512]
+        g.remote_dma(ap, ap, sem["c%d" % r], sem.lsem, pid, rid, topo.mask(core, T.cores[q]))
+    for k in range(1, len(pcs)):
+        send_piece(k)
+    nl = 3 * noff + len(pcs) * len(spare)
+    gi_b = inc(g.iota(T.iod[:], [[1, 128]], 0, -1, allow_small_or_imprecise_dtypes=True), "gi")
+
+    def relayout(e):
+        for hl in range(2):
+            Y.dma_start(T.ctab[hl::16, e * 4096:(e + 1) * 4096],
+                        T.land[:, e * 512 + hl * 256:e * 512 + hl * 256 + 256]).then_inc(sem.rl, 16)
+
+    Y.wait_ge(sem.v, n_qo)
+    Y.wait_ge(sem.s, s_qo)
+    relayout(r)
+    Y.wait_ge(sem["c%d" % far], noff)
+    relayout(far)
+    Y.wait_ge(sem.v, n_qb)
+    Y.wait_ge(sem["c%d" % plane], noff)
+    relayout(plane)
+    Y.wait_ge(sem.s, s_qc)
+    Y.wait_ge(sem["c%d" % mate], noff)
+    relayout(mate)
+
+    V.wait_ge(sem.gi, gi_a)
+    v(V.tensor_scalar(T.pint[:, 0:1], T.pidx[:, 0:1], 15, None, A.bitwise_and))
+    n = v(V.tensor_scalar(T.pint[:, 1:2], T.pidx[:, 0:1], 4, None, A.arith_shift_right))
+    V.wait_ge(sem.ldv, 32)
+    for k in range(6):
+        n_b = v(V.tensor_scalar(T.bits[:, 32 * k:32 * k + 32], T.dayb[:], 5 - k, 1, A.arith_shift_right, A.bitwise_and))
+    n_t0 = v(V.tensor_scalar(T.t0[:], T.verb[:], 2.0, -BIG, A.mult, A.add))
+    vw(n)
+    n = v(V.tensor_copy(T.pflt[:, 0:2], T.pint[:, 0:2]))
+    vw(n)
+    v(V.tensor_tensor(T.s0[:], T.t0[:], T.bits[:, 0:32], A.add))
+    v(V.tensor_scalar(T.kk[:], T.bits[:], BIG - 1.0 - HUGE, HUGE, A.mult, A.add))
+    v(V.tensor_scalar(T.pflt[:, 2:3], T.pflt[:, 0:1], 15.0, BIG, A.is_equal, A.mult))
+    v(V.tensor_scalar(T.bd[:], T.iom[:], T.pflt[:, 1:2], 2.0, A.is_equal, A.mult))
+    v(V.tensor_scalar(T.sa[:], T.ioi[:], T.pflt[:, 0:1], BIG, A.is_equal, A.mult))
+    n = v(V.tensor_scalar(T.sb[:], T.ioi[:], T.pflt[:, 0:1], -BIG, A.is_lt, A.mult))
+    vw(n)
+    v(V.tensor_scalar(T.woff[:, 0:32], T.s0[:], BIG, None, A.add))
+    v(V.tensor_tensor(T.uu[:, 0:32], T.s0[:], T.kk[:, 0:32], A.add))
+    v(V.tensor_scalar(T.pflt[:, 3:4], T.pflt[:, 2:3], -2.0 * BIG, None, A.add))
+    n = v(V.tensor_tensor(T.spat[:, 0:256], T.sa[:], T.sb[:], A.add))
+    vw(n)
+    v(V.tensor_scalar(T.soff[:, 0:32], T.uu[:, 0:32], 0.5, float(ZCOL), A.mult, A.min))
+    n = v(V.tensor_copy(T.spat[:, 256:512], T.spat[:, 0:256]))
+    vw(n)
+    v(V.tensor_scalar(T.spat[:, 15::16], T.bits[:, 32:64], T.pflt[:, 3:4], None, A.add))
+    V.wait_ge(sem.gi, gi_b)
+    n_pre = v(V.tensor_scalar(T.ident[:], T.iod[:], 0.0, None, A.is_equal))
+
+    pw = [T.pw0, T.pw1]
+    pa = [T.pa0, T.pa1]
+    for k in range(len(pcs)):
+        S.wait_ge(sem["ld%d" % k], 16)
+    S.wait_ge(sem.v, n_pre)
+    S.wait_ge(sem.rl, 8 * 16)
+    ready = [n_pre, n_pre]
+    upd = [n_pre, n_pre]
+    n_so = {0: n_pre}
+    last = [0, 0]
+    for l in range(5):
+        for s in range(2):
+            S.wait_ge(sem.v, ready[s])
+            c0 = 32 * l + 16 * s
+            ns = inc(S.activation(T.gat[:, 256 * s:256 * s + 256], T.ctab[:, :].indirect(T.woff[:, c0:c0 + 16]), F.Copy), "s")
+            P.wait_ge(sem.s, ns)
+            npe = inc(P.matmul(pw[s][:, 0:256], T.bd[:], T.gat[:, 256 * s:256 * s + 256], True, True), "p")
+            V.wait_ge(sem.p, npe)
+            vw(upd[s])
+            o = 512 * l + 256 * s
+            n = v(V.tensor_tensor_scan(T.scn[:, o:o + 256], pw[s][:, 0:256], T.spat[:, 256 * s:256 * s + 256], -1.0, A.max, A.add))
+            vw(n)
+            c1 = c0 + 32
+            pick = T.scn[:, o + 15:o + 256:16]
+            if l < 4:
+                ready[s] = v(V.tensor_scalar(T.woff[:, c1:c1 + 16], pick, BIG, None, A.add))
+                upd[s] = v(V.tensor_scalar(T.spat[:, 256 * s + 15:256 * s + 256:16], T.bits[:, c1 + 32:c1 + 48], T.pflt[:, 3:4], None, A.add))
+                if s == 1:
+                    a = 32 * (l + 1)
+                    n = v(V.tensor_tensor(T.uu[:, a:a + 32], T.scn[:, 512 * l + 15:512 * l + 512:16], T.kk[:, a:a + 32], A.add))
+                    vw(n)
+                    n_so[l + 1] = v(V.tensor_scalar(T.soff[:, a:a + 32], T.uu[:, a:a + 32], 0.5, float(ZCOL), A.mult, A.min))
+            else:
+                n = v(V.tensor_tensor(T.uu[:, c1:c1 + 16], pick, T.kk[:, c1:c1 + 16], A.add))
+                vw(n)
+                last[s] = v(V.tensor_scalar(T.soff[:, c1:c1 + 16], T.uu[:, c1:c1 + 16], 0.5, float(ZCOL), A.mult, A.min))
+
+    narr = 3 * len(pcs) * noff
+    win = T.swin[:, :]
+
+    def so(k, s):
+        return T.soff[:, 32 * k + 16 * s:32 * k + 16 * s + 16]
+
+    S.wait_ge(sem.sarr, narr)
+    S.wait_ge(sem.v, n_so[2])
+    done = [0, 0]
+    for s in range(2):
+        for k in range(3):
+            o = 768 * s + 256 * k
+            ns = inc(S.activation(T.gs[:, o:o + 256], win.indirect(so(k, s)), F.Copy), "s")
+            P.wait_ge(sem.s, ns)
+            ins = P.matmul(pa[s][:, 0:256], T.ident[:], T.gs[:, o:o + 256], k == 0, k == 2)
+            if k == 2:
+                done[s] = inc(ins, "p")
+    V.wait_ge(sem.sarr, narr)
+    vw(last[1])
+    for s in range(2):
+        ac = T.acc[:, 256 * s:256 * s + 256]
+        n = v(V.tensor_copy(ac, win.indirect(so(3, s))))
+        for k in (4, 5):
+            vw(n)
+            n = v(V.tensor_tensor(ac, win.indirect(so(k, s)), ac, A.add))
+        vw(n)
+        V.wait_ge(sem.p, done[s])
+        n = v(V.tensor_tensor(T.ysb[:, 256 * s:256 * s + 256], ac, pa[s][:, 0:256], A.add))
+        Y.wait_ge(sem.v, n)
+        Y.dma_start(T.y[:, 256 * s:256 * s + 256], T.ysb[:, 256 * s:256 * s + 256]).then_inc(sem.st, 16)
+    g.wait_ge(sem.lsem, nl)
+    Y.wait_ge(sem.s, cnt["s"])
+    Y.wait_ge(sem.st, 32)

@@ -2,50 +2,56 @@ from concourse.bass import DstId, RemoteDMATransfer
 from concourse.mybir import AluOpType as A, ActivationFunctionType as F
 
 ND = 2048
-BIG = 16384.0
-HUGE = 65536.0
-ZCOL = 8192
-PIECES = [(0, 128), (1, 320), (2, 320), (0, 384), (1, 320), (2, 320), (0, 256)]
+PAD = 8
+OFF = 16384.0
+PIECES = [
+    (128, "mate", "PA0", "SB0", "SB1", "off"),
+    (256, "plane", "SA0", "PB0", "PB1", "on"),
+    (256, "mate", "PA0", "SB1", "SB0", "on"),
+    (256, "plane", "SA1", "PB1", "PB0", "on"),
+    (256, "mate", "PA0", "SB0", "SB1", "all"),
+    (256, "plane", "SA0", "PB0", "PB1", "all"),
+    (256, "mate", "PA0", "SB1", "SB0", "all"),
+    (256, "plane", "SA1", "PB1", "PB0", "all"),
+    (128, "mate", "PA0", "SA0", "SA1", "all"),
+]
+LOADS = [[0], [1, 2], [3, 4], [5, 6], [7, 8]]
+HOP = 3
 
 SCRATCH = {
-    "swin": ("sbuf", [128, 8200], "float32"),
+    "swin": ("sbuf", [128, PAD + 4 * ND], "float32"),
     "ctab": ("sbuf", [128, 16384], "bfloat16"),
     "land": ("sbuf", [128, 2048], "bfloat16"),
     "chi": ("sbuf", [128, 256], "int32"),
-    "zt": ("sbuf", [128, 512], "bfloat16"),
     "verb": ("sbuf", [128, 32], "int32"),
     "dayb": ("sbuf", [128, 32], "int32"),
-    "pidx": ("sbuf", [128, 4], "int32"),
-    "pint": ("sbuf", [128, 4], "int32"),
-    "pflt": ("sbuf", [128, 4], "float32"),
-    "ioi": ("sbuf", [128, 256], "float32"),
-    "iom": ("sbuf", [128, 128], "float32"),
-    "iod": ("sbuf", [128, 128], "float32"),
-    "bd": ("sbuf", [128, 128], "bfloat16"),
+    "ones": ("sbuf", [128, 128], "float32"),
     "ident": ("sbuf", [128, 128], "float32"),
-    "sa": ("sbuf", [128, 256], "float32"),
-    "sb": ("sbuf", [128, 256], "float32"),
-    "spat": ("sbuf", [128, 512], "float32"),
+    "twos": ("sbuf", [128, 16], "float32"),
+    "pick": ("sbuf", [128, 144], "bfloat16"),
     "bits": ("sbuf", [128, 192], "int32"),
-    "kk": ("sbuf", [128, 192], "float32"),
+    "inj": ("sbuf", [128, 192], "float32"),
+    "kk": ("sbuf", [128, 160], "float32"),
     "t0": ("sbuf", [128, 32], "float32"),
-    "s0": ("sbuf", [128, 32], "float32"),
-    "uu": ("sbuf", [128, 192], "float32"),
+    "x0": ("sbuf", [128, 32], "float32"),
+    "uu": ("sbuf", [128, 160], "float32"),
     "woff": ("sbuf", [128, 160], "uint16"),
     "soff": ("sbuf", [128, 192], "uint16"),
     "gat": ("sbuf", [128, 512], "bfloat16"),
-    "scn": ("sbuf", [128, 2560], "float32"),
-    "gs": ("sbuf", [128, 1536], "float32"),
+    "gs": ("sbuf", [128, 1280], "float32"),
     "acc": ("sbuf", [128, 512], "float32"),
     "ysb": ("sbuf", [128, 512], "float32"),
-    "pw0": ("psum", [128, 512], "float32"),
     "pw1": ("psum", [128, 512], "float32"),
+    "pw2": ("psum", [128, 512], "float32"),
+    "pw3": ("psum", [128, 512], "float32"),
+    "pw4": ("psum", [128, 512], "float32"),
+    "pw5": ("psum", [128, 512], "float32"),
     "pa0": ("psum", [128, 512], "float32"),
     "pa1": ("psum", [128, 512], "float32"),
 }
 SEMAPHORES = (["v", "s", "p", "gi", "ldc", "ldv", "rl", "sarr", "lsem", "st"]
-              + ["ld%d" % k for k in range(len(PIECES))]
-              + ["h%d" % k for k in range(len(PIECES))]
+              + ["ld%d" % k for k in range(len(LOADS))]
+              + ["h%d_%d" % (r, k) for r in range(4) for k in range(len(PIECES))]
               + ["c%d" % k for k in range(4)])
 
 
@@ -56,29 +62,38 @@ def bits_of(engs):
     return m
 
 
-def layout(T, topo, r):
+def peers(T, topo, r):
     me = T.cores[r]
-    mate = plane = far = None
+    out = {}
     for q, c in enumerate(T.cores):
-        if q == r:
-            continue
-        if topo.mates(topo.chip(me), topo.chip(c)):
-            mate = q
-        elif topo.same_plane(topo.chip(me), topo.chip(c)):
-            plane = q
-        else:
-            far = q
-    others = [c for c in topo.cores_of(me) if c != me]
-    port = [c for c in others if topo.may_write(c, T.cores[mate])]
-    port.sort(key=lambda c: topo.die(c) != topo.die(me))
-    rest = [c for c in others if c not in port]
-    side = []
-    for c in port:
-        d = [x for x in rest if topo.die(x) == topo.die(c) and x not in side][0]
-        side.append(d)
-    off = topo.engines(me, T.cores[mate])
-    spare = [e for e in topo.engines(me, others[0]) if e not in off]
-    return mate, plane, far, port, side, spare
+        if q != r:
+            if topo.mates(topo.chip(me), topo.chip(c)):
+                out["mate"] = q
+            elif topo.same_plane(topo.chip(me), topo.chip(c)):
+                out["plane"] = q
+            else:
+                out["far"] = q
+    return out
+
+
+def helpers(T, topo, r):
+    me = T.cores[r]
+    mate = T.cores[peers(T, topo, r)["mate"]]
+    out, n = {}, {}
+    for c in topo.cores_of(me):
+        if c != me:
+            kind = ("P" if topo.may_write(c, mate) else "S") + ("A" if topo.die(c) == topo.die(me) else "B")
+            out["%s%d" % (kind, n.get(kind, 0))] = c
+            n[kind] = n.get(kind, 0) + 1
+    return out
+
+
+def engine_sets(topo, core, T):
+    away = [c for c in T.cores if topo.chip(c) != topo.chip(core) and topo.may_write(core, c)][0]
+    near = [c for c in topo.cores_of(core) if c != core][0]
+    off = topo.engines(core, away)
+    every = topo.engines(core, near)
+    return {"off": off, "all": every, "on": [e for e in every if e not in off]}
 
 
 def dst(topo, c):
@@ -87,39 +102,48 @@ def dst(topo, c):
 
 
 def piece_cols(r):
-    out, a = [], r * ND
-    for h, w in PIECES:
-        out.append((h, a, a + w))
-        a += w
+    out, a = [], PAD + r * ND
+    for p in PIECES:
+        out.append((a, a + p[0]))
+        a += p[0]
     return out
+
+
+def tree(T, topo, r, k):
+    _, kind, first, relay, local, how = PIECES[k]
+    pr = peers(T, topo, r)
+    via, other = (pr["mate"], pr["plane"]) if kind == "mate" else (pr["plane"], pr["mate"])
+    own, there = helpers(T, topo, r), helpers(T, topo, via)
+    return [(own[first], 0, how, there[relay], own[local]),
+            (there[relay], 1, "off", T.cores[pr["far"]], T.cores[via]),
+            (own[local], 1, "on", T.cores[other], None)]
 
 
 def helper_program(g, core, T, topo):
     sem = T.sem
-    for r, me in enumerate(T.cores):
-        if topo.chip(me) != topo.chip(core):
-            continue
-        mate, plane, far, port, side, spare = layout(T, topo, r)
-        n = 0
-        for k, (h, a, b) in enumerate(piece_cols(r)):
-            ap = T.swin[:, a:b]
-            if core == port[h]:
-                g.wait_ge(sem["h%d" % k], len(spare))
-                m = topo.mask(core, T.cores[mate])
-                g.remote_dma_fused([
-                    RemoteDMATransfer(dst_ids=[dst(topo, T.cores[far]), dst(topo, T.cores[mate])], dma_engine_mask=m,
-                                      remote_sem=sem.sarr, srcs=[ap], dsts=[ap, ap]),
-                    RemoteDMATransfer(dst_ids=[dst(topo, side[h])], dma_engine_mask=bits_of(spare),
-                                      remote_sem=sem["h%d" % k], srcs=[ap], dsts=[ap]),
-                ], local_sem=sem.lsem)
-                n += len(topo.engines(core, T.cores[mate])) + len(spare)
-            elif core == side[h]:
-                g.wait_ge(sem["h%d" % k], len(spare))
-                rid, pid, _ = topo.addr(T.cores[plane])
-                g.remote_dma(ap, ap, sem.sarr, sem.lsem, pid, rid, topo.mask(core, T.cores[plane]))
-                n += len(topo.engines(core, T.cores[plane]))
-        if n:
-            g.wait_ge(sem.lsem, n)
+    todo = []
+    for r in range(len(T.cores)):
+        for k in range(len(PIECES)):
+            for c, depth, how, away, near in tree(T, topo, r, k):
+                if c == core:
+                    todo.append((k + HOP * depth, -depth, r, k, how, away, near))
+    if not todo:
+        return
+    eng = engine_sets(topo, core, T)
+    n = 0
+    for _, _, r, k, how, away, near in sorted(todo):
+        a, b = piece_cols(r)[k]
+        ap = T.swin[:, a:b]
+        h = sem["h%d_%d" % (r, k)]
+        g.wait_ge(h, len(eng[how]))
+        tr = []
+        for c, e in ((away, "off"), (near, "on")):
+            if c is not None:
+                tr.append(RemoteDMATransfer(dst_ids=[dst(topo, c)], dma_engine_mask=bits_of(eng[e]),
+                                            remote_sem=sem.sarr if c in T.cores else h, srcs=[ap], dsts=[ap]))
+                n += len(eng[e])
+        g.remote_dma_fused(tr, local_sem=sem.lsem)
+    g.wait_ge(sem.lsem, n)
 
 
 def rank_program(g, core, T, topo):
@@ -129,185 +153,204 @@ def rank_program(g, core, T, topo):
         return
     sem = T.sem
     V, S, P, Y = g.vector, g.scalar, g.tensor, g.sync
-    mate, plane, far, port, side, spare = layout(T, topo, r)
-    noff = len(topo.engines(core, T.cores[mate]))
+    Q = {"v": V, "s": S, "p": P, "gi": g, "y": Y}
+    pr = peers(T, topo, r)
+    mate, plane, far = pr["mate"], pr["plane"], pr["far"]
+    eng = engine_sets(topo, core, T)
+    noff = len(eng["off"])
     pcs = piece_cols(r)
     cnt = {"v": 0, "s": 0, "p": 0, "gi": 0}
+    seen = {}
 
-    def inc(ins, name):
-        ins.then_inc(sem[name], 1)
-        cnt[name] += 1
-        return cnt[name]
+    def wait(q, *toks):
+        for name, n in toks:
+            if seen.get((q, name), 0) < n:
+                Q[q].wait_ge(sem[name], n)
+                seen[(q, name)] = n
 
-    def v(ins):
-        return inc(ins, "v")
-
-    def vw(n):
-        V.wait_ge(sem.v, n)
+    def done(q, ins):
+        ins.then_inc(sem[q], 1)
+        cnt[q] += 1
+        return (q, cnt[q])
 
     def quarter(e, a=0, b=4096):
         return T.ctab[:, e * 4096 + a:e * 4096 + b]
 
+    def cols(t, k, a=0, b=32):
+        return t[:, 32 * k + a:32 * k + b]
+
     Y.dma_start(T.chi[:], T.child[:]).then_inc(sem.ldc, 16)
-    for k, (h, a, b) in enumerate(pcs):
-        q = S if k % 2 == 0 else Y
-        q.dma_start(T.swin[:, a:b], T.sums[:, a - r * ND:b - r * ND]).then_inc(sem["ld%d" % k], 16)
+    load_of = {}
+    for i, ks in enumerate(LOADS):
+        a, b = pcs[ks[0]][0], pcs[ks[-1]][1]
+        q = S if i % 2 == 0 else Y
+        q.dma_start(T.swin[:, a:b], T.sums[:, a - pcs[0][0]:b - pcs[0][0]]).then_inc(sem["ld%d" % i], 16)
+        for k in ks:
+            load_of[k] = ("ld%d" % i, 16)
     Y.dma_start(T.verb[:], T.ver[:]).then_inc(sem.ldv, 16)
     Y.dma_start(T.dayb[:], T.day[:]).then_inc(sem.ldv, 16)
 
-    inc(g.iota(T.pidx[:, 0:1], [[0, 1]], 0, 1), "gi")
-    inc(g.iota(T.ioi[:], [[0, 16], [1, 16]], 0, 0, allow_small_or_imprecise_dtypes=True), "gi")
-    gi_a = inc(g.iota(T.iom[:], [[1, 8], [0, 16]], 0, 0, allow_small_or_imprecise_dtypes=True), "gi")
-
-    n_z = v(V.memset(T.zt[:], 0.0))
-    n_qa = v(V.memset(quarter(far), 0.0))
-    V.wait_ge(sem.ldc, 16)
+    g_fill = done("gi", g.iota(quarter(mate, 1024, 1792), [[0, 768]], 0, 0, allow_small_or_imprecise_dtypes=True))
+    v_src = done("v", V.memset(quarter(mate, 0, 1024), 0.0))
+    done("v", V.memset(quarter(r, 0, 3072), 0.0))
+    wait("v", ("ldc", 16))
     own = r * 512
-    n = v(V.tensor_copy(T.land[:, own:own + 256], T.chi[:]))
-    vw(n)
-    n_prep = v(V.tensor_tensor(T.land[:, own + 256:own + 512], T.chi[:], T.land[:, own:own + 256], A.subtract))
-    n_qo = v(V.memset(quarter(r, 0, 2048), 0.0))
-    n_qb = v(V.memset(quarter(plane), 0.0))
-    v(V.memset(T.swin[:, ZCOL:ZCOL + 8], 0.0))
-
-    S.wait_ge(sem.v, n_z)
+    t = done("v", V.tensor_copy(T.land[:, own:own + 256], T.chi[:]))
+    wait("v", t)
+    v_prep = done("v", V.tensor_tensor(T.land[:, own + 256:own + 512], T.chi[:], T.land[:, own:own + 256], A.subtract))
+    v_own = done("v", V.memset(quarter(r, 3072, 4096), 0.0))
+    v_z = done("v", V.memset(T.pick[:], 0.0))
+    v_plane = done("v", V.memset(quarter(plane), 0.0))
+    v_mate = done("v", V.memset(quarter(mate, 1792, 2816), 0.0))
+    done("v", V.memset(T.swin[:, 0:PAD], 0.0))
+    wait("s", v_src)
     for j in range(4):
-        s_qo = inc(S.activation(quarter(r, 2048 + 512 * j, 2560 + 512 * j), T.zt[:], F.Copy), "s")
-    for j in range(8):
-        s_qc = inc(S.activation(quarter(mate, 512 * j, 512 * j + 512), T.zt[:], F.Copy), "s")
+        s_far = done("s", S.activation(quarter(far, 1024 * j, 1024 * j + 1024), quarter(mate, 0, 1024), F.Copy))
+    done("s", S.activation(quarter(mate, 2816, 3456), quarter(mate, 0, 640), F.Copy))
+    s_mate = done("s", S.activation(quarter(mate, 3456, 4096), quarter(mate, 0, 640), F.Copy))
 
-    nl = 0
+    own_helpers = helpers(T, topo, r)
+    nl = [0]
 
     def send_piece(k):
-        h, a, b = pcs[k]
-        g.wait_ge(sem["ld%d" % k], 16)
-        rid, pid, _ = topo.addr(port[h])
-        g.remote_dma(T.swin[:, a:b], T.swin[:, a:b], sem["h%d" % k], sem.lsem, pid, rid, bits_of(spare))
+        a, b = pcs[k]
+        wait("gi", load_of[k])
+        rid, pid, _ = topo.addr(own_helpers[PIECES[k][2]])
+        e = eng[PIECES[k][5]]
+        g.remote_dma(T.swin[:, a:b], T.swin[:, a:b], sem["h%d_%d" % (r, k)], sem.lsem, pid, rid, bits_of(e))
+        nl[0] += len(e)
 
     send_piece(0)
-    g.wait_ge(sem.v, n_prep)
-    for q in (far, plane, mate):
-        rid, pid, _ = topo.addr(T.cores[q])
-        ap = T.land[:, own:own + 512]
-        g.remote_dma(ap, ap, sem["c%d" % r], sem.lsem, pid, rid, topo.mask(core, T.cores[q]))
+    wait("gi", v_prep)
+    ap = T.land[:, own:own + 512]
+    g.remote_dma_fused([RemoteDMATransfer(dst_ids=[dst(topo, T.cores[q]) for q in (far, plane, mate)],
+                                          dma_engine_mask=bits_of(eng["off"]), remote_sem=sem["c%d" % r],
+                                          srcs=[ap], dsts=[ap, ap, ap])], local_sem=sem.lsem)
+    nl[0] += noff
     for k in range(1, len(pcs)):
         send_piece(k)
-    nl = 3 * noff + len(pcs) * len(spare)
-    gi_b = inc(g.iota(T.iod[:], [[1, 128]], 0, -1, allow_small_or_imprecise_dtypes=True), "gi")
+    done("gi", g.iota(T.twos[:, 0:8], [[0, 8]], 2, 0, allow_small_or_imprecise_dtypes=True))
+    t = done("gi", g.iota(T.ones[:], [[0, 128]], 1, 0, allow_small_or_imprecise_dtypes=True))
+    wait("gi", t)
+    t = done("gi", g.affine_select(T.twos[:, 8:16], T.twos[:, 0:8], [[-16, 8]], A.is_ge, 0.0, 0, 1))
+    g_id = done("gi", g.affine_select(T.ident[:], T.ones[:], [[-1, 128]], A.is_equal, 0.0, 0, 1))
+    wait("gi", t, v_z)
+    g_pick = done("gi", g.affine_select(T.pick[:, 15:128:16], T.twos[:, 8:16], [[16, 8]], A.is_ge, 0.0, 15, -1))
 
-    def relayout(e):
-        for hl in range(2):
-            Y.dma_start(T.ctab[hl::16, e * 4096:(e + 1) * 4096],
-                        T.land[:, e * 512 + hl * 256:e * 512 + hl * 256 + 256]).then_inc(sem.rl, 16)
+    def relayout(q, e, hl):
+        Q[q].dma_start(T.ctab[hl::16, e * 4096:(e + 1) * 4096],
+                       T.land[:, e * 512 + hl * 256:e * 512 + hl * 256 + 256]).then_inc(sem.rl, 16)
 
-    Y.wait_ge(sem.v, n_qo)
-    Y.wait_ge(sem.s, s_qo)
-    relayout(r)
-    Y.wait_ge(sem["c%d" % far], noff)
-    relayout(far)
-    Y.wait_ge(sem.v, n_qb)
-    Y.wait_ge(sem["c%d" % plane], noff)
-    relayout(plane)
-    Y.wait_ge(sem.s, s_qc)
-    Y.wait_ge(sem["c%d" % mate], noff)
-    relayout(mate)
+    wait("y", v_own)
+    relayout("y", r, 0)
+    relayout("y", r, 1)
+    wait("y", s_far, ("c%d" % far, noff))
+    relayout("y", far, 0)
+    relayout("y", far, 1)
+    wait("y", v_plane, ("c%d" % plane, noff))
+    relayout("y", plane, 0)
+    relayout("y", plane, 1)
+    for hl, q in enumerate("ys"):
+        wait(q, v_mate, s_mate, g_fill, ("c%d" % mate, noff))
+        relayout(q, mate, hl)
 
-    V.wait_ge(sem.gi, gi_a)
-    v(V.tensor_scalar(T.pint[:, 0:1], T.pidx[:, 0:1], 15, None, A.bitwise_and))
-    n = v(V.tensor_scalar(T.pint[:, 1:2], T.pidx[:, 0:1], 4, None, A.arith_shift_right))
-    V.wait_ge(sem.ldv, 32)
+    wait("v", ("ldv", 32))
     for k in range(6):
-        n_b = v(V.tensor_scalar(T.bits[:, 32 * k:32 * k + 32], T.dayb[:], 5 - k, 1, A.arith_shift_right, A.bitwise_and))
-    n_t0 = v(V.tensor_scalar(T.t0[:], T.verb[:], 2.0, -BIG, A.mult, A.add))
-    vw(n)
-    n = v(V.tensor_copy(T.pflt[:, 0:2], T.pint[:, 0:2]))
-    vw(n)
-    v(V.tensor_tensor(T.s0[:], T.t0[:], T.bits[:, 0:32], A.add))
-    v(V.tensor_scalar(T.kk[:], T.bits[:], BIG - 1.0 - HUGE, HUGE, A.mult, A.add))
-    v(V.tensor_scalar(T.pflt[:, 2:3], T.pflt[:, 0:1], 15.0, BIG, A.is_equal, A.mult))
-    v(V.tensor_scalar(T.bd[:], T.iom[:], T.pflt[:, 1:2], 2.0, A.is_equal, A.mult))
-    v(V.tensor_scalar(T.sa[:], T.ioi[:], T.pflt[:, 0:1], BIG, A.is_equal, A.mult))
-    n = v(V.tensor_scalar(T.sb[:], T.ioi[:], T.pflt[:, 0:1], -BIG, A.is_lt, A.mult))
-    vw(n)
-    v(V.tensor_scalar(T.woff[:, 0:32], T.s0[:], BIG, None, A.add))
-    v(V.tensor_tensor(T.uu[:, 0:32], T.s0[:], T.kk[:, 0:32], A.add))
-    v(V.tensor_scalar(T.pflt[:, 3:4], T.pflt[:, 2:3], -2.0 * BIG, None, A.add))
-    n = v(V.tensor_tensor(T.spat[:, 0:256], T.sa[:], T.sb[:], A.add))
-    vw(n)
-    v(V.tensor_scalar(T.soff[:, 0:32], T.uu[:, 0:32], 0.5, float(ZCOL), A.mult, A.min))
-    n = v(V.tensor_copy(T.spat[:, 256:512], T.spat[:, 0:256]))
-    vw(n)
-    v(V.tensor_scalar(T.spat[:, 15::16], T.bits[:, 32:64], T.pflt[:, 3:4], None, A.add))
-    V.wait_ge(sem.gi, gi_b)
-    n_pre = v(V.tensor_scalar(T.ident[:], T.iod[:], 0.0, None, A.is_equal))
+        t = done("v", V.tensor_scalar(cols(T.bits, k), T.dayb[:], 5 - k, 1, A.arith_shift_right, A.bitwise_and))
+    t = done("v", V.tensor_scalar(T.t0[:], T.verb[:], 2.0, None, A.mult))
+    wait("v", t)
+    v_x0 = done("v", V.tensor_tensor(T.x0[:], T.t0[:], cols(T.bits, 0), A.add))
+    done("v", V.tensor_copy(T.inj[:, 32:160], T.bits[:, 32:160]))
+    v_inj = done("v", V.tensor_scalar(cols(T.inj, 5), cols(T.bits, 5), 2 * PAD + OFF, -OFF, A.mult, A.add))
+    v_kk = done("v", V.tensor_scalar(T.kk[:], T.bits[:, 0:160], 2 * PAD - 1 + OFF, -OFF, A.mult, A.add))
+    wait("v", v_x0)
+    ready = done("v", V.tensor_copy(cols(T.woff, 0), T.x0[:]))
+    wait("v", v_kk)
 
-    pw = [T.pw0, T.pw1]
-    pa = [T.pa0, T.pa1]
-    for k in range(len(pcs)):
-        S.wait_ge(sem["ld%d" % k], 16)
-    S.wait_ge(sem.v, n_pre)
-    S.wait_ge(sem.rl, 8 * 16)
-    ready = [n_pre, n_pre]
-    upd = [n_pre, n_pre]
-    n_so = {0: n_pre}
-    last = [0, 0]
-    for l in range(5):
-        for s in range(2):
-            S.wait_ge(sem.v, ready[s])
-            c0 = 32 * l + 16 * s
-            ns = inc(S.activation(T.gat[:, 256 * s:256 * s + 256], T.ctab[:, :].indirect(T.woff[:, c0:c0 + 16]), F.Copy), "s")
-            P.wait_ge(sem.s, ns)
-            npe = inc(P.matmul(pw[s][:, 0:256], T.bd[:], T.gat[:, 256 * s:256 * s + 256], True, True), "p")
-            V.wait_ge(sem.p, npe)
-            vw(upd[s])
-            o = 512 * l + 256 * s
-            n = v(V.tensor_tensor_scan(T.scn[:, o:o + 256], pw[s][:, 0:256], T.spat[:, 256 * s:256 * s + 256], -1.0, A.max, A.add))
-            vw(n)
-            c1 = c0 + 32
-            pick = T.scn[:, o + 15:o + 256:16]
-            if l < 4:
-                ready[s] = v(V.tensor_scalar(T.woff[:, c1:c1 + 16], pick, BIG, None, A.add))
-                upd[s] = v(V.tensor_scalar(T.spat[:, 256 * s + 15:256 * s + 256:16], T.bits[:, c1 + 32:c1 + 48], T.pflt[:, 3:4], None, A.add))
-                if s == 1:
-                    a = 32 * (l + 1)
-                    n = v(V.tensor_tensor(T.uu[:, a:a + 32], T.scn[:, 512 * l + 15:512 * l + 512:16], T.kk[:, a:a + 32], A.add))
-                    vw(n)
-                    n_so[l + 1] = v(V.tensor_scalar(T.soff[:, a:a + 32], T.uu[:, a:a + 32], 0.5, float(ZCOL), A.mult, A.min))
-            else:
-                n = v(V.tensor_tensor(T.uu[:, c1:c1 + 16], pick, T.kk[:, c1:c1 + 16], A.add))
-                vw(n)
-                last[s] = v(V.tensor_scalar(T.soff[:, c1:c1 + 16], T.uu[:, c1:c1 + 16], 0.5, float(ZCOL), A.mult, A.min))
-
-    narr = 3 * len(pcs) * noff
+    pw = {k: T["pw%d" % k][:, 0:32] for k in range(1, 6)}
+    pw[0] = T.x0[:]
+    pa = [T.pa0[:, 0:256], T.pa1[:, 0:256]]
+    wait("p", g_id, v_inj)
+    for k in range(1, 6):
+        P.matmul(pw[k], T.ident[:], cols(T.inj, k), True, False)
+    wait("p", g_pick)
+    so = {}
     win = T.swin[:, :]
+    sums_in = [("sarr", 3 * len(pcs) * noff)] + [("ld%d" % i, 16) for i in range(len(LOADS))]
+    accd = [None, None]
+    slot = [0]
 
-    def so(k, s):
-        return T.soff[:, 32 * k + 16 * s:32 * k + 16 * s + 16]
+    def sum_offsets(k):
+        t = done("v", V.tensor_tensor(cols(T.uu, k), pw[k], cols(T.kk, k), A.add))
+        wait("v", t)
+        so[k] = done("v", V.tensor_scalar(cols(T.soff, k), cols(T.uu, k), 0.5, 0.0, A.mult, A.max))
 
-    S.wait_ge(sem.sarr, narr)
-    S.wait_ge(sem.v, n_so[2])
-    done = [0, 0]
-    for s in range(2):
-        for k in range(3):
-            o = 768 * s + 256 * k
-            ns = inc(S.activation(T.gs[:, o:o + 256], win.indirect(so(k, s)), F.Copy), "s")
-            P.wait_ge(sem.s, ns)
-            ins = P.matmul(pa[s][:, 0:256], T.ident[:], T.gs[:, o:o + 256], k == 0, k == 2)
-            if k == 2:
-                done[s] = inc(ins, "p")
-    V.wait_ge(sem.sarr, narr)
-    vw(last[1])
-    for s in range(2):
-        ac = T.acc[:, 256 * s:256 * s + 256]
-        n = v(V.tensor_copy(ac, win.indirect(so(3, s))))
-        for k in (4, 5):
-            vw(n)
-            n = v(V.tensor_tensor(ac, win.indirect(so(k, s)), ac, A.add))
-        vw(n)
-        V.wait_ge(sem.p, done[s])
-        n = v(V.tensor_tensor(T.ysb[:, 256 * s:256 * s + 256], ac, pa[s][:, 0:256], A.add))
-        Y.wait_ge(sem.v, n)
-        Y.dma_start(T.y[:, 256 * s:256 * s + 256], T.ysb[:, 256 * s:256 * s + 256]).then_inc(sem.st, 16)
-    g.wait_ge(sem.lsem, nl)
-    Y.wait_ge(sem.s, cnt["s"])
-    Y.wait_ge(sem.st, 32)
+    def half(t, h):
+        return t[:, 256 * h:256 * h + 256]
+
+    def src(k, h):
+        return win.indirect(cols(T.soff, k, 16 * h, 16 * h + 16))
+
+    def v_job(k, h):
+        wait("v", so[k], *sums_in)
+        if accd[h] is None:
+            accd[h] = done("v", V.tensor_copy(half(T.acc, h), src(k, h)))
+        else:
+            wait("v", accd[h])
+            accd[h] = done("v", V.tensor_tensor(half(T.acc, h), src(k, h), half(T.acc, h), A.add))
+
+    def s_job(k, h):
+        wait("s", so[k], *sums_in)
+        out = half(T.gs, slot[0])
+        slot[0] += 1
+        return out, done("s", S.activation(out, src(k, h), F.Copy))
+
+    def p_add(job, h, start, stop):
+        wait("p", job[1])
+        ins = P.matmul(pa[h], T.ident[:], job[0], start, stop)
+        return done("p", ins) if stop else None
+
+    def finish(h, part):
+        wait("v", accd[h], part)
+        t = done("v", V.tensor_tensor(half(T.ysb, h), half(T.acc, h), pa[h], A.add))
+        wait("y", t)
+        Y.dma_start(half(T.y, h), half(T.ysb, h)).then_inc(sem.st, 16)
+
+    def step(l, vcols):
+        toks = []
+        if vcols:
+            wait("v", ready, ("rl", 128))
+            toks.append(done("v", V.tensor_copy(T.gat[:, 0:16 * vcols], T.ctab[:, :].indirect(cols(T.woff, l, 0, vcols)))))
+        wait("s", ready, ("rl", 128))
+        toks.append(done("s", S.activation(T.gat[:, 16 * vcols:512], T.ctab[:, :].indirect(cols(T.woff, l, vcols, 32)), F.Copy)))
+        wait("p", *toks)
+        for i in range(16):
+            ins = P.matmul(pw[l + 1], T.pick[:, 15 - i:143 - i], T.gat[:, i::16], False, i == 15)
+        return done("p", ins)
+
+    for l in range(4):
+        picked = step(l, 16)
+        sum_offsets(l)
+        if l == 3:
+            v_job(0, 0)
+            b0, b1 = s_job(0, 1), s_job(1, 1)
+            p_add(b0, 1, True, False)
+            p_add(b1, 1, False, False)
+        wait("v", picked)
+        ready = done("v", V.tensor_copy(cols(T.woff, l + 1), pw[l + 1]))
+    picked = step(4, 0)
+    b2, a1, a2 = s_job(2, 1), s_job(1, 0), s_job(2, 0)
+    part_b = p_add(b2, 1, False, True)
+    p_add(a1, 0, True, False)
+    part_a = p_add(a2, 0, False, True)
+    sum_offsets(4)
+    for k, h in ((3, 0), (4, 0), (3, 1), (4, 1)):
+        v_job(k, h)
+    wait("v", picked)
+    so[5] = done("v", V.tensor_scalar(cols(T.soff, 5), pw[5], 0.5, 0.0, A.mult, A.max))
+    v_job(5, 1)
+    finish(1, part_b)
+    v_job(5, 0)
+    finish(0, part_a)
+    g.wait_ge(sem.lsem, nl[0])
+    wait("y", ("s", cnt["s"]), ("gi", cnt["gi"]), ("st", 32))

@@ -5,18 +5,22 @@ ND = 2048
 PAD = 8
 OFF = 16384.0
 PIECES = [
-    (128, "mate", "PA0", "SB0", "SB1", "off"),
-    (256, "plane", "SA0", "PB0", "PB1", "on"),
-    (256, "mate", "PA0", "SB1", "SB0", "on"),
-    (256, "plane", "SA1", "PB1", "PB0", "on"),
-    (256, "mate", "PA0", "SB0", "SB1", "all"),
-    (256, "plane", "SA0", "PB0", "PB1", "all"),
-    (256, "mate", "PA0", "SB1", "SB0", "all"),
-    (256, "plane", "SA1", "PB1", "PB0", "all"),
-    (128, "mate", "PA0", "SA0", "SA1", "all"),
+    (256, "mate", "PA0", "SB1", "SB1", "off"),
+    (256, "plane", "SB0", "PB1", "PB0", "on"),
+    (256, "mate", "PB1", "SB0", "SB1", "on0"),
+    (256, "plane", "SA1", "PB0", "PA0", "on1"),
+    (256, "mate", "PA0", "SB0", "SA1", "on0"),
+    (256, "plane", "SA0", "PB1", "PB0", "on1"),
+    (256, "plane", "SA0", "PB0", "PA0", "off"),
+    (256, "plane", "SA1", "PA0", "PB1", "on"),
 ]
-LOADS = [[0], [1, 2], [3, 4], [5, 6], [7, 8]]
-HOP = 3
+CALLS = [[0, 1], [2, 3], [4, 5], [6, 7]]
+LOADS = [("s", [0]), ("s", [1]), ("y", [2, 3])]
+START = [0, 1, 2, 3]
+LAG = {"first": 0, "local": 1.9, "relay": 3.1}
+SCALAR = [(0, 0), (0, 1), (1, 0), (2, 0), (1, 1), (2, 1)]
+START_SUM = (0, 1)
+VECTOR = [(3, 0), ("last", 0), (4, 0), ("last", 1), (5, 0), (3, 1), (4, 1), ("store", 0), (5, 1), ("store", 1)]
 
 SCRATCH = {
     "swin": ("sbuf", [128, PAD + 4 * ND], "float32"),
@@ -30,7 +34,8 @@ SCRATCH = {
     "twos": ("sbuf", [128, 16], "float32"),
     "pick": ("sbuf", [128, 144], "bfloat16"),
     "bits": ("sbuf", [128, 192], "int32"),
-    "inj": ("sbuf", [128, 192], "float32"),
+    "identb": ("sbuf", [128, 128], "bfloat16"),
+    "inj": ("sbuf", [128, 192], "bfloat16"),
     "kk": ("sbuf", [128, 160], "float32"),
     "t0": ("sbuf", [128, 32], "float32"),
     "x0": ("sbuf", [128, 32], "float32"),
@@ -38,9 +43,10 @@ SCRATCH = {
     "woff": ("sbuf", [128, 160], "uint16"),
     "soff": ("sbuf", [128, 192], "uint16"),
     "gat": ("sbuf", [128, 512], "bfloat16"),
-    "gs": ("sbuf", [128, 1280], "float32"),
+    "gs": ("sbuf", [128, 2048], "float32"),
     "acc": ("sbuf", [128, 512], "float32"),
     "ysb": ("sbuf", [128, 512], "float32"),
+    "pw0": ("psum", [128, 512], "float32"),
     "pw1": ("psum", [128, 512], "float32"),
     "pw2": ("psum", [128, 512], "float32"),
     "pw3": ("psum", [128, 512], "float32"),
@@ -52,7 +58,7 @@ SCRATCH = {
 SEMAPHORES = (["v", "s", "p", "gi", "ldc", "ldv", "rl", "sarr", "lsem", "st"]
               + ["ld%d" % k for k in range(len(LOADS))]
               + ["h%d_%d" % (r, k) for r in range(4) for k in range(len(PIECES))]
-              + ["c%d" % k for k in range(4)])
+              + ["c%d" % r for r in range(4)])
 
 
 def bits_of(engs):
@@ -93,7 +99,8 @@ def engine_sets(topo, core, T):
     near = [c for c in topo.cores_of(core) if c != core][0]
     off = topo.engines(core, away)
     every = topo.engines(core, near)
-    return {"off": off, "all": every, "on": [e for e in every if e not in off]}
+    on = [e for e in every if e not in off]
+    return {**{"e%d" % i: every[2 * i:2 * i + 2] for i in range(len(every) // 2)}, "hoff": off, "hon": on, "off": off, "all": every, "on": on, "on0": on[0::2], "on1": on[1::2], "off0": off[0::2], "off1": off[1::2]}
 
 
 def dst(topo, c):
@@ -114,33 +121,38 @@ def tree(T, topo, r, k):
     pr = peers(T, topo, r)
     via, other = (pr["mate"], pr["plane"]) if kind == "mate" else (pr["plane"], pr["mate"])
     own, there = helpers(T, topo, r), helpers(T, topo, via)
-    return [(own[first], 0, how, there[relay], own[local]),
-            (there[relay], 1, "off", T.cores[pr["far"]], T.cores[via]),
-            (own[local], 1, "on", T.cores[other], None)]
+    if local is None:
+        return [(own[first], "first", how, there[relay], None),
+                (there[relay], "relay", "off", T.cores[pr["far"]], T.cores[via])]
+    return [(own[first], "first", how, there[relay], own[local]),
+            (there[relay], "relay", "hoff", T.cores[pr["far"]], T.cores[via]),
+            (own[local], "local", "hon", T.cores[other], None)]
+
+
+def child_part(T, r, hl):
+    return T.land[:, r * 512 + hl * 256:r * 512 + hl * 256 + 256]
 
 
 def helper_program(g, core, T, topo):
     sem = T.sem
     todo = []
     for r in range(len(T.cores)):
-        for k in range(len(PIECES)):
-            for c, depth, how, away, near in tree(T, topo, r, k):
+        for k, (a, b) in enumerate(piece_cols(r)):
+            for c, role, how, away, near in tree(T, topo, r, k):
                 if c == core:
-                    todo.append((k + HOP * depth, -depth, r, k, how, away, near))
+                    at = START[[k in ks for ks in CALLS].index(True)] + LAG[role]
+                    todo.append((at, len(todo), T.swin[:, a:b], "h%d_%d" % (r, k), "sarr", how, away, near))
     if not todo:
         return
     eng = engine_sets(topo, core, T)
     n = 0
-    for _, _, r, k, how, away, near in sorted(todo):
-        a, b = piece_cols(r)[k]
-        ap = T.swin[:, a:b]
-        h = sem["h%d_%d" % (r, k)]
-        g.wait_ge(h, len(eng[how]))
+    for _, _, ap, h, end, how, away, near in sorted(todo, key=lambda x: x[:2]):
+        g.wait_ge(sem[h], len(eng[how]))
         tr = []
-        for c, e in ((away, "off"), (near, "on")):
+        for c, e in ((away, "hoff"), (near, "hon")):
             if c is not None:
                 tr.append(RemoteDMATransfer(dst_ids=[dst(topo, c)], dma_engine_mask=bits_of(eng[e]),
-                                            remote_sem=sem.sarr if c in T.cores else h, srcs=[ap], dsts=[ap]))
+                                            remote_sem=sem[end if c in T.cores else h], srcs=[ap], dsts=[ap]))
                 n += len(eng[e])
         g.remote_dma_fused(tr, local_sem=sem.lsem)
     g.wait_ge(sem.lsem, n)
@@ -180,78 +192,80 @@ def rank_program(g, core, T, topo):
         return t[:, 32 * k + a:32 * k + b]
 
     Y.dma_start(T.chi[:], T.child[:]).then_inc(sem.ldc, 16)
-    load_of = {}
-    for i, ks in enumerate(LOADS):
-        a, b = pcs[ks[0]][0], pcs[ks[-1]][1]
-        q = S if i % 2 == 0 else Y
-        q.dma_start(T.swin[:, a:b], T.sums[:, a - pcs[0][0]:b - pcs[0][0]]).then_inc(sem["ld%d" % i], 16)
-        for k in ks:
-            load_of[k] = ("ld%d" % i, 16)
+    for i, (q, calls) in enumerate(LOADS):
+        a, b = pcs[CALLS[calls[0]][0]][0], pcs[CALLS[calls[-1]][-1]][1]
+        Q[q].dma_start(T.swin[:, a:b], T.sums[:, a - pcs[0][0]:b - pcs[0][0]]).then_inc(sem["ld%d" % i], 16)
     Y.dma_start(T.verb[:], T.ver[:]).then_inc(sem.ldv, 16)
     Y.dma_start(T.dayb[:], T.day[:]).then_inc(sem.ldv, 16)
 
-    g_fill = done("gi", g.iota(quarter(mate, 1024, 1792), [[0, 768]], 0, 0, allow_small_or_imprecise_dtypes=True))
+    done("v", V.memset(T.pick[:], 0.0))
+    done("v", V.memset(T.twos[:, 0:8], 2.0))
+    v_ones = done("v", V.memset(T.ones[:], 1.0))
     v_src = done("v", V.memset(quarter(mate, 0, 1024), 0.0))
-    done("v", V.memset(quarter(r, 0, 3072), 0.0))
+    done("v", V.memset(quarter(r, 0, 1024), 0.0))
     wait("v", ("ldc", 16))
-    own = r * 512
-    t = done("v", V.tensor_copy(T.land[:, own:own + 256], T.chi[:]))
-    wait("v", t)
-    v_prep = done("v", V.tensor_tensor(T.land[:, own + 256:own + 512], T.chi[:], T.land[:, own:own + 256], A.subtract))
-    v_own = done("v", V.memset(quarter(r, 3072, 4096), 0.0))
-    v_z = done("v", V.memset(T.pick[:], 0.0))
+    v_hi = done("v", V.tensor_copy(child_part(T, r, 0), T.chi[:]))
+    wait("v", v_hi)
+    v_lo = done("v", V.tensor_tensor(child_part(T, r, 1), T.chi[:], child_part(T, r, 0), A.subtract))
+    v_own = done("v", V.memset(quarter(r, 1024, 4096), 0.0))
     v_plane = done("v", V.memset(quarter(plane), 0.0))
-    v_mate = done("v", V.memset(quarter(mate, 1792, 2816), 0.0))
+    v_mate = done("v", V.memset(quarter(mate, 1024, 2560), 0.0))
     done("v", V.memset(T.swin[:, 0:PAD], 0.0))
     wait("s", v_src)
     for j in range(4):
         s_far = done("s", S.activation(quarter(far, 1024 * j, 1024 * j + 1024), quarter(mate, 0, 1024), F.Copy))
-    done("s", S.activation(quarter(mate, 2816, 3456), quarter(mate, 0, 640), F.Copy))
-    s_mate = done("s", S.activation(quarter(mate, 3456, 4096), quarter(mate, 0, 640), F.Copy))
+    done("s", S.activation(quarter(mate, 2560, 3328), quarter(mate, 0, 768), F.Copy))
+    s_mate = done("s", S.activation(quarter(mate, 3328, 4096), quarter(mate, 0, 768), F.Copy))
 
-    own_helpers = helpers(T, topo, r)
     nl = [0]
 
-    def send_piece(k):
-        a, b = pcs[k]
-        wait("gi", load_of[k])
-        rid, pid, _ = topo.addr(own_helpers[PIECES[k][2]])
-        e = eng[PIECES[k][5]]
-        g.remote_dma(T.swin[:, a:b], T.swin[:, a:b], sem["h%d_%d" % (r, k)], sem.lsem, pid, rid, bits_of(e))
-        nl[0] += len(e)
+    def hand_on(i):
+        wait("gi", ("ld%d" % [i in calls for _, calls in LOADS].index(True), 16))
+        tr = []
+        for k in CALLS[i]:
+            ap = T.swin[:, pcs[k][0]:pcs[k][1]]
+            for c, role, how, _, _ in tree(T, topo, r, k):
+                if role in ("first", "relay0", "local0"):
+                    tr.append(RemoteDMATransfer(dst_ids=[dst(topo, c)], dma_engine_mask=bits_of(eng[how]),
+                                                remote_sem=sem["h%d_%d" % (r, k)], srcs=[ap], dsts=[ap]))
+                    nl[0] += len(eng[how])
+        g.remote_dma_fused(tr, local_sem=sem.lsem)
 
-    send_piece(0)
-    wait("gi", v_prep)
-    ap = T.land[:, own:own + 512]
+    wait("gi", v_ones)
+    t = done("gi", g.affine_select(T.twos[:, 8:16], T.twos[:, 0:8], [[-16, 8]], A.is_ge, 0.0, 0, 1))
+    g_id = done("gi", g.affine_select(T.ident[:], T.ones[:], [[-1, 128]], A.is_equal, 0.0, 0, 1))
+    wait("gi", t)
+    g_pick = done("gi", g.affine_select(T.pick[:, 15:128:16], T.twos[:, 8:16], [[16, 8]], A.is_ge, 0.0, 15, -1))
+    hand_on(0)
+    wait("gi", v_lo)
+    ap = T.land[:, r * 512:r * 512 + 512]
     g.remote_dma_fused([RemoteDMATransfer(dst_ids=[dst(topo, T.cores[q]) for q in (far, plane, mate)],
                                           dma_engine_mask=bits_of(eng["off"]), remote_sem=sem["c%d" % r],
                                           srcs=[ap], dsts=[ap, ap, ap])], local_sem=sem.lsem)
     nl[0] += noff
-    for k in range(1, len(pcs)):
-        send_piece(k)
-    done("gi", g.iota(T.twos[:, 0:8], [[0, 8]], 2, 0, allow_small_or_imprecise_dtypes=True))
-    t = done("gi", g.iota(T.ones[:], [[0, 128]], 1, 0, allow_small_or_imprecise_dtypes=True))
-    wait("gi", t)
-    t = done("gi", g.affine_select(T.twos[:, 8:16], T.twos[:, 0:8], [[-16, 8]], A.is_ge, 0.0, 0, 1))
-    g_id = done("gi", g.affine_select(T.ident[:], T.ones[:], [[-1, 128]], A.is_equal, 0.0, 0, 1))
-    wait("gi", t, v_z)
-    g_pick = done("gi", g.affine_select(T.pick[:, 15:128:16], T.twos[:, 8:16], [[16, 8]], A.is_ge, 0.0, 15, -1))
+    for i in range(1, len(CALLS)):
+        hand_on(i)
+    for k, p in enumerate(PIECES):
+        if p[4] is None:
+            ap = T.swin[:, pcs[k][0]:pcs[k][1]]
+            rid, pid, _ = topo.addr(T.cores[mate])
+            g.remote_dma(ap, ap, sem.sarr, sem.lsem, pid, rid, bits_of(eng["off"]))
+            nl[0] += noff
 
     def relayout(q, e, hl):
-        Q[q].dma_start(T.ctab[hl::16, e * 4096:(e + 1) * 4096],
-                       T.land[:, e * 512 + hl * 256:e * 512 + hl * 256 + 256]).then_inc(sem.rl, 16)
+        if e != r:
+            wait(q, ("c%d" % e, noff))
+        Q[q].dma_start(T.ctab[hl::16, e * 4096:(e + 1) * 4096], child_part(T, e, hl)).then_inc(sem.rl, 16)
 
     wait("y", v_own)
     relayout("y", r, 0)
     relayout("y", r, 1)
-    wait("y", s_far, ("c%d" % far, noff))
-    relayout("y", far, 0)
-    relayout("y", far, 1)
-    wait("y", v_plane, ("c%d" % plane, noff))
-    relayout("y", plane, 0)
-    relayout("y", plane, 1)
     for hl, q in enumerate("ys"):
-        wait(q, v_mate, s_mate, g_fill, ("c%d" % mate, noff))
+        wait(q, s_far)
+        relayout(q, far, hl)
+        wait(q, v_plane)
+        relayout(q, plane, hl)
+        wait(q, v_mate, s_mate)
         relayout(q, mate, hl)
 
     wait("v", ("ldv", 32))
@@ -260,6 +274,8 @@ def rank_program(g, core, T, topo):
     t = done("v", V.tensor_scalar(T.t0[:], T.verb[:], 2.0, None, A.mult))
     wait("v", t)
     v_x0 = done("v", V.tensor_tensor(T.x0[:], T.t0[:], cols(T.bits, 0), A.add))
+    wait("v", g_id)
+    done("v", V.tensor_copy(T.identb[:], T.ident[:]))
     done("v", V.tensor_copy(T.inj[:, 32:160], T.bits[:, 32:160]))
     v_inj = done("v", V.tensor_scalar(cols(T.inj, 5), cols(T.bits, 5), 2 * PAD + OFF, -OFF, A.mult, A.add))
     v_kk = done("v", V.tensor_scalar(T.kk[:], T.bits[:, 0:160], 2 * PAD - 1 + OFF, -OFF, A.mult, A.add))
@@ -267,23 +283,27 @@ def rank_program(g, core, T, topo):
     ready = done("v", V.tensor_copy(cols(T.woff, 0), T.x0[:]))
     wait("v", v_kk)
 
-    pw = {k: T["pw%d" % k][:, 0:32] for k in range(1, 6)}
-    pw[0] = T.x0[:]
+    def hcols(t, k, h):
+        return cols(t, k, 16 * h, 16 * h + 16)
+
+    def pw(k, h):
+        return T["pw%d" % (2 * (k % 3) + h)][:, 0:16] if k else hcols(T.x0, 0, h)
+
+    def inject(k, h):
+        P.matmul(pw(k, h), T.identb[:], hcols(T.inj, k, h), True, False)
+
     pa = [T.pa0[:, 0:256], T.pa1[:, 0:256]]
-    wait("p", g_id, v_inj)
-    for k in range(1, 6):
-        P.matmul(pw[k], T.ident[:], cols(T.inj, k), True, False)
+    wait("p", v_inj)
+    for k in range(1, 4):
+        inject(k, 0)
+        inject(k, 1)
     wait("p", g_pick)
+    ready, picked = [ready, ready], [None, None]
     so = {}
     win = T.swin[:, :]
-    sums_in = [("sarr", 3 * len(pcs) * noff)] + [("ld%d" % i, 16) for i in range(len(LOADS))]
+    sums_in = [("sarr", len(pcs) * (len(eng["hon"]) + 2 * len(eng["hoff"])))] + [("ld%d" % i, 16) for i in range(len(LOADS))]
     accd = [None, None]
     slot = [0]
-
-    def sum_offsets(k):
-        t = done("v", V.tensor_tensor(cols(T.uu, k), pw[k], cols(T.kk, k), A.add))
-        wait("v", t)
-        so[k] = done("v", V.tensor_scalar(cols(T.soff, k), cols(T.uu, k), 0.5, 0.0, A.mult, A.max))
 
     def half(t, h):
         return t[:, 256 * h:256 * h + 256]
@@ -292,7 +312,7 @@ def rank_program(g, core, T, topo):
         return win.indirect(cols(T.soff, k, 16 * h, 16 * h + 16))
 
     def v_job(k, h):
-        wait("v", so[k], *sums_in)
+        wait("v", so[k, h], *sums_in)
         if accd[h] is None:
             accd[h] = done("v", V.tensor_copy(half(T.acc, h), src(k, h)))
         else:
@@ -300,7 +320,7 @@ def rank_program(g, core, T, topo):
             accd[h] = done("v", V.tensor_tensor(half(T.acc, h), src(k, h), half(T.acc, h), A.add))
 
     def s_job(k, h):
-        wait("s", so[k], *sums_in)
+        wait("s", so[k, h], *sums_in)
         out = half(T.gs, slot[0])
         slot[0] += 1
         return out, done("s", S.activation(out, src(k, h), F.Copy))
@@ -316,41 +336,46 @@ def rank_program(g, core, T, topo):
         wait("y", t)
         Y.dma_start(half(T.y, h), half(T.ysb, h)).then_inc(sem.st, 16)
 
-    def step(l, vcols):
-        toks = []
-        if vcols:
-            wait("v", ready, ("rl", 128))
-            toks.append(done("v", V.tensor_copy(T.gat[:, 0:16 * vcols], T.ctab[:, :].indirect(cols(T.woff, l, 0, vcols)))))
-        wait("s", ready, ("rl", 128))
-        toks.append(done("s", S.activation(T.gat[:, 16 * vcols:512], T.ctab[:, :].indirect(cols(T.woff, l, vcols, 32)), F.Copy)))
-        wait("p", *toks)
+    def step(l, h):
+        if l:
+            wait("v", picked[h])
+            ready[h] = done("v", V.tensor_copy(hcols(T.woff, l, h), pw(l, h)))
+        a = 16 * h
+        wait("v", ready[h], ("rl", 128))
+        tv = done("v", V.tensor_copy(T.gat[:, 16 * a:16 * a + 128], T.ctab[:, :].indirect(cols(T.woff, l, a, a + 8))))
+        wait("s", ready[h], ("rl", 128))
+        ts = done("s", S.activation(T.gat[:, 16 * a + 128:16 * a + 256],
+                                    T.ctab[:, :].indirect(cols(T.woff, l, a + 8, a + 16)), F.Copy))
+        if l >= 3:
+            wait("p", so[l - 2, h])
+            inject(l + 1, h)
+        wait("p", tv, ts)
         for i in range(16):
-            ins = P.matmul(pw[l + 1], T.pick[:, 15 - i:143 - i], T.gat[:, i::16], False, i == 15)
-        return done("p", ins)
+            ins = P.matmul(pw(l + 1, h), T.pick[:, 15 - i:143 - i], T.gat[:, 16 * a + i:16 * a + 256:16], False, i == 15)
+        picked[h] = done("p", ins)
+        t = done("v", V.tensor_tensor(hcols(T.uu, l, h), pw(l, h), hcols(T.kk, l, h), A.add))
+        if h:
+            wait("v", t)
+            so[l, 0] = so[l, 1] = done("v", V.tensor_scalar(cols(T.soff, l), cols(T.uu, l), 0.5, 0.0, A.mult, A.max))
 
-    for l in range(4):
-        picked = step(l, 16)
-        sum_offsets(l)
-        if l == 3:
-            v_job(0, 0)
-            b0, b1 = s_job(0, 1), s_job(1, 1)
-            p_add(b0, 1, True, False)
-            p_add(b1, 1, False, False)
-        wait("v", picked)
-        ready = done("v", V.tensor_copy(cols(T.woff, l + 1), pw[l + 1]))
-    picked = step(4, 0)
-    b2, a1, a2 = s_job(2, 1), s_job(1, 0), s_job(2, 0)
-    part_b = p_add(b2, 1, False, True)
-    p_add(a1, 0, True, False)
-    part_a = p_add(a2, 0, False, True)
-    sum_offsets(4)
-    for k, h in ((3, 0), (4, 0), (3, 1), (4, 1)):
-        v_job(k, h)
-    wait("v", picked)
-    so[5] = done("v", V.tensor_scalar(cols(T.soff, 5), pw[5], 0.5, 0.0, A.mult, A.max))
-    v_job(5, 1)
-    finish(1, part_b)
-    v_job(5, 0)
-    finish(0, part_a)
+    for l in range(5):
+        step(l, 0)
+        step(l, 1)
+    jobs, part = {}, {}
+    for k, h in SCALAR:
+        if (k, h) == START_SUM:
+            wait("s", so[k, h], *sums_in)
+            accd[h] = done("s", S.activation(half(T.acc, h), src(k, h), F.Copy))
+        else:
+            mine = [j for j in SCALAR if j[1] == h and j != START_SUM]
+            part[h] = p_add(s_job(k, h), h, (k, h) == mine[0], (k, h) == mine[-1])
+    for k, h in VECTOR:
+        if k == "last":
+            wait("v", picked[h])
+            so[5, h] = done("v", V.tensor_scalar(hcols(T.soff, 5, h), pw(5, h), 0.5, 0.0, A.mult, A.max))
+        elif k == "store":
+            finish(h, part[h])
+        else:
+            v_job(k, h)
     g.wait_ge(sem.lsem, nl[0])
     wait("y", ("s", cnt["s"]), ("gi", cnt["gi"]), ("st", 32))

from concourse.bass import DstId, RemoteDMATransfer
from concourse.mybir import AluOpType as A, ActivationFunctionType as F

ND = 2048
PAD = 8
OFF = 16384.0
PIECES = [
    (256, "mate", "PA0", "SB1", "SB1", "off"),
    (256, "plane", "SB0", "PB1", "PB0", "on"),
    (256, "mate", "PB1", "SB0", "SB1", "on0"),
    (256, "plane", "SA1", "PB0", "PA0", "on1"),
    (256, "mate", "PA0", "SB0", "SA1", "on0"),
    (256, "plane", "SA0", "PB1", "PB0", "on1"),
    (256, "plane", "SA0", "PB0", "PA0", "off"),
    (256, "plane", "SA1", "PA0", "PB1", "on"),
]
CALLS = [[0, 1], [2, 3], [4, 5], [6, 7]]
LOADS = [("s", [0]), ("s", [1]), ("y", [2, 3])]
START = [0, 1, 2, 3]
LAG = {"first": 0, "local": 1.9, "relay": 3.1}
SCALAR = [(0, 0), (0, 1), (1, 0), (2, 0), (1, 1), (2, 1)]
START_SUM = (0, 1)
VECTOR = [(3, 0), ("last", 0), (4, 0), ("last", 1), (5, 0), (3, 1), (4, 1), ("store", 0), (5, 1), ("store", 1)]

SCRATCH = {
    "swin": ("sbuf", [128, PAD + 4 * ND], "float32"),
    "ctab": ("sbuf", [128, 16384], "bfloat16"),
    "land": ("sbuf", [128, 2048], "bfloat16"),
    "chi": ("sbuf", [128, 256], "int32"),
    "verb": ("sbuf", [128, 32], "int32"),
    "dayb": ("sbuf", [128, 32], "int32"),
    "ones": ("sbuf", [128, 128], "float32"),
    "ident": ("sbuf", [128, 128], "float32"),
    "twos": ("sbuf", [128, 16], "float32"),
    "pick": ("sbuf", [128, 144], "bfloat16"),
    "bits": ("sbuf", [128, 192], "int32"),
    "identb": ("sbuf", [128, 128], "bfloat16"),
    "inj": ("sbuf", [128, 192], "bfloat16"),
    "kk": ("sbuf", [128, 160], "float32"),
    "t0": ("sbuf", [128, 32], "float32"),
    "x0": ("sbuf", [128, 32], "float32"),
    "uu": ("sbuf", [128, 160], "float32"),
    "woff": ("sbuf", [128, 160], "uint16"),
    "soff": ("sbuf", [128, 192], "uint16"),
    "gat": ("sbuf", [128, 512], "bfloat16"),
    "gs": ("sbuf", [128, 2048], "float32"),
    "acc": ("sbuf", [128, 512], "float32"),
    "ysb": ("sbuf", [128, 512], "float32"),
    "pw0": ("psum", [128, 512], "float32"),
    "pw1": ("psum", [128, 512], "float32"),
    "pw2": ("psum", [128, 512], "float32"),
    "pw3": ("psum", [128, 512], "float32"),
    "pw4": ("psum", [128, 512], "float32"),
    "pw5": ("psum", [128, 512], "float32"),
    "pa0": ("psum", [128, 512], "float32"),
    "pa1": ("psum", [128, 512], "float32"),
}
SEMAPHORES = (["v", "s", "p", "gi", "ldc", "ldv", "rl", "sarr", "lsem", "st"]
              + ["ld%d" % k for k in range(len(LOADS))]
              + ["h%d_%d" % (r, k) for r in range(4) for k in range(len(PIECES))]
              + ["c%d" % r for r in range(4)])


def bits_of(engs):
    m = 0
    for e in engs:
        m |= 1 << e
    return m


def peers(T, topo, r):
    me = T.cores[r]
    out = {}
    for q, c in enumerate(T.cores):
        if q != r:
            if topo.mates(topo.chip(me), topo.chip(c)):
                out["mate"] = q
            elif topo.same_plane(topo.chip(me), topo.chip(c)):
                out["plane"] = q
            else:
                out["far"] = q
    return out


def helpers(T, topo, r):
    me = T.cores[r]
    mate = T.cores[peers(T, topo, r)["mate"]]
    out, n = {}, {}
    for c in topo.cores_of(me):
        if c != me:
            kind = ("P" if topo.may_write(c, mate) else "S") + ("A" if topo.die(c) == topo.die(me) else "B")
            out["%s%d" % (kind, n.get(kind, 0))] = c
            n[kind] = n.get(kind, 0) + 1
    return out


def engine_sets(topo, core, T):
    away = [c for c in T.cores if topo.chip(c) != topo.chip(core) and topo.may_write(core, c)][0]
    near = [c for c in topo.cores_of(core) if c != core][0]
    off = topo.engines(core, away)
    every = topo.engines(core, near)
    on = [e for e in every if e not in off]
    return {**{"e%d" % i: every[2 * i:2 * i + 2] for i in range(len(every) // 2)}, "hoff": off, "hon": on, "off": off, "all": every, "on": on, "on0": on[0::2], "on1": on[1::2], "off0": off[0::2], "off1": off[1::2]}


def dst(topo, c):
    rid, pid, _ = topo.addr(c)
    return DstId(rid=rid, pnc=pid)


def piece_cols(r):
    out, a = [], PAD + r * ND
    for p in PIECES:
        out.append((a, a + p[0]))
        a += p[0]
    return out


def tree(T, topo, r, k):
    _, kind, first, relay, local, how = PIECES[k]
    pr = peers(T, topo, r)
    via, other = (pr["mate"], pr["plane"]) if kind == "mate" else (pr["plane"], pr["mate"])
    own, there = helpers(T, topo, r), helpers(T, topo, via)
    if local is None:
        return [(own[first], "first", how, there[relay], None),
                (there[relay], "relay", "off", T.cores[pr["far"]], T.cores[via])]
    return [(own[first], "first", how, there[relay], own[local]),
            (there[relay], "relay", "hoff", T.cores[pr["far"]], T.cores[via]),
            (own[local], "local", "hon", T.cores[other], None)]


def child_part(T, r, hl):
    return T.land[:, r * 512 + hl * 256:r * 512 + hl * 256 + 256]


def helper_program(g, core, T, topo):
    sem = T.sem
    todo = []
    for r in range(len(T.cores)):
        for k, (a, b) in enumerate(piece_cols(r)):
            for c, role, how, away, near in tree(T, topo, r, k):
                if c == core:
                    at = START[[k in ks for ks in CALLS].index(True)] + LAG[role]
                    todo.append((at, len(todo), T.swin[:, a:b], "h%d_%d" % (r, k), "sarr", how, away, near))
    if not todo:
        return
    eng = engine_sets(topo, core, T)
    n = 0
    for _, _, ap, h, end, how, away, near in sorted(todo, key=lambda x: x[:2]):
        g.wait_ge(sem[h], len(eng[how]))
        tr = []
        for c, e in ((away, "hoff"), (near, "hon")):
            if c is not None:
                tr.append(RemoteDMATransfer(dst_ids=[dst(topo, c)], dma_engine_mask=bits_of(eng[e]),
                                            remote_sem=sem[end if c in T.cores else h], srcs=[ap], dsts=[ap]))
                n += len(eng[e])
        g.remote_dma_fused(tr, local_sem=sem.lsem)
    g.wait_ge(sem.lsem, n)


def rank_program(g, core, T, topo):
    r = T.rank_of(core)
    if r is None:
        helper_program(g, core, T, topo)
        return
    sem = T.sem
    V, S, P, Y = g.vector, g.scalar, g.tensor, g.sync
    Q = {"v": V, "s": S, "p": P, "gi": g, "y": Y}
    pr = peers(T, topo, r)
    mate, plane, far = pr["mate"], pr["plane"], pr["far"]
    eng = engine_sets(topo, core, T)
    noff = len(eng["off"])
    pcs = piece_cols(r)
    cnt = {"v": 0, "s": 0, "p": 0, "gi": 0}
    seen = {}

    def wait(q, *toks):
        for name, n in toks:
            if seen.get((q, name), 0) < n:
                Q[q].wait_ge(sem[name], n)
                seen[(q, name)] = n

    def done(q, ins):
        ins.then_inc(sem[q], 1)
        cnt[q] += 1
        return (q, cnt[q])

    def quarter(e, a=0, b=4096):
        return T.ctab[:, e * 4096 + a:e * 4096 + b]

    def cols(t, k, a=0, b=32):
        return t[:, 32 * k + a:32 * k + b]

    Y.dma_start(T.chi[:], T.child[:]).then_inc(sem.ldc, 16)
    for i, (q, calls) in enumerate(LOADS):
        a, b = pcs[CALLS[calls[0]][0]][0], pcs[CALLS[calls[-1]][-1]][1]
        Q[q].dma_start(T.swin[:, a:b], T.sums[:, a - pcs[0][0]:b - pcs[0][0]]).then_inc(sem["ld%d" % i], 16)
    Y.dma_start(T.verb[:], T.ver[:]).then_inc(sem.ldv, 16)
    Y.dma_start(T.dayb[:], T.day[:]).then_inc(sem.ldv, 16)

    done("v", V.memset(T.pick[:], 0.0))
    done("v", V.memset(T.twos[:, 0:8], 2.0))
    v_ones = done("v", V.memset(T.ones[:], 1.0))
    v_src = done("v", V.memset(quarter(mate, 0, 1024), 0.0))
    done("v", V.memset(quarter(r, 0, 1024), 0.0))
    wait("v", ("ldc", 16))
    v_hi = done("v", V.tensor_copy(child_part(T, r, 0), T.chi[:]))
    wait("v", v_hi)
    v_lo = done("v", V.tensor_tensor(child_part(T, r, 1), T.chi[:], child_part(T, r, 0), A.subtract))
    v_own = done("v", V.memset(quarter(r, 1024, 4096), 0.0))
    v_plane = done("v", V.memset(quarter(plane), 0.0))
    v_mate = done("v", V.memset(quarter(mate, 1024, 2560), 0.0))
    done("v", V.memset(T.swin[:, 0:PAD], 0.0))
    wait("s", v_src)
    for j in range(4):
        s_far = done("s", S.activation(quarter(far, 1024 * j, 1024 * j + 1024), quarter(mate, 0, 1024), F.Copy))
    done("s", S.activation(quarter(mate, 2560, 3328), quarter(mate, 0, 768), F.Copy))
    s_mate = done("s", S.activation(quarter(mate, 3328, 4096), quarter(mate, 0, 768), F.Copy))

    nl = [0]

    def hand_on(i):
        wait("gi", ("ld%d" % [i in calls for _, calls in LOADS].index(True), 16))
        tr = []
        for k in CALLS[i]:
            ap = T.swin[:, pcs[k][0]:pcs[k][1]]
            for c, role, how, _, _ in tree(T, topo, r, k):
                if role in ("first", "relay0", "local0"):
                    tr.append(RemoteDMATransfer(dst_ids=[dst(topo, c)], dma_engine_mask=bits_of(eng[how]),
                                                remote_sem=sem["h%d_%d" % (r, k)], srcs=[ap], dsts=[ap]))
                    nl[0] += len(eng[how])
        g.remote_dma_fused(tr, local_sem=sem.lsem)

    wait("gi", v_ones)
    t = done("gi", g.affine_select(T.twos[:, 8:16], T.twos[:, 0:8], [[-16, 8]], A.is_ge, 0.0, 0, 1))
    g_id = done("gi", g.affine_select(T.ident[:], T.ones[:], [[-1, 128]], A.is_equal, 0.0, 0, 1))
    wait("gi", t)
    g_pick = done("gi", g.affine_select(T.pick[:, 15:128:16], T.twos[:, 8:16], [[16, 8]], A.is_ge, 0.0, 15, -1))
    hand_on(0)
    wait("gi", v_lo)
    ap = T.land[:, r * 512:r * 512 + 512]
    g.remote_dma_fused([RemoteDMATransfer(dst_ids=[dst(topo, T.cores[q]) for q in (far, plane, mate)],
                                          dma_engine_mask=bits_of(eng["off"]), remote_sem=sem["c%d" % r],
                                          srcs=[ap], dsts=[ap, ap, ap])], local_sem=sem.lsem)
    nl[0] += noff
    for i in range(1, len(CALLS)):
        hand_on(i)
    for k, p in enumerate(PIECES):
        if p[4] is None:
            ap = T.swin[:, pcs[k][0]:pcs[k][1]]
            rid, pid, _ = topo.addr(T.cores[mate])
            g.remote_dma(ap, ap, sem.sarr, sem.lsem, pid, rid, bits_of(eng["off"]))
            nl[0] += noff

    def relayout(q, e, hl):
        if e != r:
            wait(q, ("c%d" % e, noff))
        Q[q].dma_start(T.ctab[hl::16, e * 4096:(e + 1) * 4096], child_part(T, e, hl)).then_inc(sem.rl, 16)

    wait("y", v_own)
    relayout("y", r, 0)
    relayout("y", r, 1)
    for hl, q in enumerate("ys"):
        wait(q, s_far)
        relayout(q, far, hl)
        wait(q, v_plane)
        relayout(q, plane, hl)
        wait(q, v_mate, s_mate)
        relayout(q, mate, hl)

    wait("v", ("ldv", 32))
    for k in range(6):
        t = done("v", V.tensor_scalar(cols(T.bits, k), T.dayb[:], 5 - k, 1, A.arith_shift_right, A.bitwise_and))
    t = done("v", V.tensor_scalar(T.t0[:], T.verb[:], 2.0, None, A.mult))
    wait("v", t)
    v_x0 = done("v", V.tensor_tensor(T.x0[:], T.t0[:], cols(T.bits, 0), A.add))
    wait("v", g_id)
    done("v", V.tensor_copy(T.identb[:], T.ident[:]))
    done("v", V.tensor_copy(T.inj[:, 32:160], T.bits[:, 32:160]))
    v_inj = done("v", V.tensor_scalar(cols(T.inj, 5), cols(T.bits, 5), 2 * PAD + OFF, -OFF, A.mult, A.add))
    v_kk = done("v", V.tensor_scalar(T.kk[:], T.bits[:, 0:160], 2 * PAD - 1 + OFF, -OFF, A.mult, A.add))
    wait("v", v_x0)
    ready = done("v", V.tensor_copy(cols(T.woff, 0), T.x0[:]))
    wait("v", v_kk)

    def hcols(t, k, h):
        return cols(t, k, 16 * h, 16 * h + 16)

    def pw(k, h):
        return T["pw%d" % (2 * (k % 3) + h)][:, 0:16] if k else hcols(T.x0, 0, h)

    def inject(k, h):
        P.matmul(pw(k, h), T.identb[:], hcols(T.inj, k, h), True, False)

    pa = [T.pa0[:, 0:256], T.pa1[:, 0:256]]
    wait("p", v_inj)
    for k in range(1, 4):
        inject(k, 0)
        inject(k, 1)
    wait("p", g_pick)
    ready, picked = [ready, ready], [None, None]
    so = {}
    win = T.swin[:, :]
    sums_in = [("sarr", len(pcs) * (len(eng["hon"]) + 2 * len(eng["hoff"])))] + [("ld%d" % i, 16) for i in range(len(LOADS))]
    accd = [None, None]
    slot = [0]

    def half(t, h):
        return t[:, 256 * h:256 * h + 256]

    def src(k, h):
        return win.indirect(cols(T.soff, k, 16 * h, 16 * h + 16))

    def v_job(k, h):
        wait("v", so[k, h], *sums_in)
        if accd[h] is None:
            accd[h] = done("v", V.tensor_copy(half(T.acc, h), src(k, h)))
        else:
            wait("v", accd[h])
            accd[h] = done("v", V.tensor_tensor(half(T.acc, h), src(k, h), half(T.acc, h), A.add))

    def s_job(k, h):
        wait("s", so[k, h], *sums_in)
        out = half(T.gs, slot[0])
        slot[0] += 1
        return out, done("s", S.activation(out, src(k, h), F.Copy))

    def p_add(job, h, start, stop):
        wait("p", job[1])
        ins = P.matmul(pa[h], T.ident[:], job[0], start, stop)
        return done("p", ins) if stop else None

    def finish(h, part):
        wait("v", accd[h], part)
        t = done("v", V.tensor_tensor(half(T.ysb, h), half(T.acc, h), pa[h], A.add))
        wait("y", t)
        Y.dma_start(half(T.y, h), half(T.ysb, h)).then_inc(sem.st, 16)

    def step(l, h):
        if l:
            wait("v", picked[h])
            ready[h] = done("v", V.tensor_copy(hcols(T.woff, l, h), pw(l, h)))
        a = 16 * h
        wait("v", ready[h], ("rl", 128))
        tv = done("v", V.tensor_copy(T.gat[:, 16 * a:16 * a + 128], T.ctab[:, :].indirect(cols(T.woff, l, a, a + 8))))
        wait("s", ready[h], ("rl", 128))
        ts = done("s", S.activation(T.gat[:, 16 * a + 128:16 * a + 256],
                                    T.ctab[:, :].indirect(cols(T.woff, l, a + 8, a + 16)), F.Copy))
        if l >= 3:
            wait("p", so[l - 2, h])
            inject(l + 1, h)
        wait("p", tv, ts)
        for i in range(16):
            ins = P.matmul(pw(l + 1, h), T.pick[:, 15 - i:143 - i], T.gat[:, 16 * a + i:16 * a + 256:16], False, i == 15)
        picked[h] = done("p", ins)
        t = done("v", V.tensor_tensor(hcols(T.uu, l, h), pw(l, h), hcols(T.kk, l, h), A.add))
        if h:
            wait("v", t)
            so[l, 0] = so[l, 1] = done("v", V.tensor_scalar(cols(T.soff, l), cols(T.uu, l), 0.5, 0.0, A.mult, A.max))

    for l in range(5):
        step(l, 0)
        step(l, 1)
    jobs, part = {}, {}
    for k, h in SCALAR:
        if (k, h) == START_SUM:
            wait("s", so[k, h], *sums_in)
            accd[h] = done("s", S.activation(half(T.acc, h), src(k, h), F.Copy))
        else:
            mine = [j for j in SCALAR if j[1] == h and j != START_SUM]
            part[h] = p_add(s_job(k, h), h, (k, h) == mine[0], (k, h) == mine[-1])
    for k, h in VECTOR:
        if k == "last":
            wait("v", picked[h])
            so[5, h] = done("v", V.tensor_scalar(hcols(T.soff, 5, h), pw(5, h), 0.5, 0.0, A.mult, A.max))
        elif k == "store":
            finish(h, part[h])
        else:
            v_job(k, h)
    g.wait_ge(sem.lsem, nl[0])
    wait("y", ("s", cnt["s"]), ("gi", cnt["gi"]), ("st", 32))
